import numpy as np, ml_dtypes
CORES = [9,10,11,14,17,18,19,22,49,50,51,54]
N = 12
TOK, K, FT = 32, 2, 4
ROUTE = [[[2,11],[6,9],[1,10],[8,9],[6,8],[3,10],[2,7],[0,3],[0,11],[5,10],[3,6],[2,7],[1,8],[4,10],[3,8],[0,11],[6,7],[5,8],[2,4],[6,7],[1,4],[0,4],[1,11],[5,11],[0,2],[2,11],[0,3],[1,10],[0,5],[0,4],[3,8],[6,7]],[[2,10],[10,11],[0,2],[2,3],[1,7],[1,2],[4,5],[4,5],[5,10],[3,6],[2,10],[5,6],[3,9],[3,11],[1,3],[6,8],[2,6],[0,6],[1,10],[9,10],[4,8],[3,5],[0,1],[4,11],[2,11],[3,11],[6,9],[3,4],[0,9],[5,11],[2,4],[1,9]],[[7,8],[7,8],[0,8],[4,7],[8,10],[0,1],[0,4],[2,7],[0,8],[8,11],[2,5],[1,9],[7,9],[4,5],[3,5],[2,3],[5,8],[1,3],[0,4],[0,2],[2,9],[2,8],[9,11],[2,4],[1,2],[2,8],[9,11],[5,6],[5,6],[7,8],[1,9],[5,11]],[[8,10],[2,6],[2,3],[0,7],[2,11],[9,11],[5,8],[4,8],[4,8],[0,6],[2,9],[1,10],[5,10],[2,10],[7,10],[3,8],[6,11],[2,5],[2,7],[2,4],[2,10],[2,7],[3,8],[5,7],[5,10],[0,11],[5,9],[9,10],[3,7],[1,11],[5,11],[1,10]],[[1,6],[2,10],[6,8],[3,4],[4,10],[3,9],[6,8],[10,11],[3,10],[4,10],[4,5],[5,9],[4,5],[1,4],[1,11],[5,11],[7,10],[1,4],[6,10],[2,10],[0,3],[6,9],[3,4],[4,11],[2,7],[3,9],[2,10],[9,11],[2,7],[2,5],[8,10],[0,5]],[[4,11],[4,8],[6,7],[3,9],[0,3],[4,10],[6,10],[1,9],[6,9],[2,4],[8,11],[1,5],[4,7],[4,10],[8,10],[9,10],[4,8],[3,4],[1,5],[3,7],[6,7],[9,11],[2,4],[1,9],[0,5],[8,11],[4,8],[3,11],[0,7],[7,10],[7,11],[2,9]],[[5,10],[1,11],[2,10],[3,6],[3,9],[3,8],[0,8],[4,6],[5,7],[7,9],[0,11],[4,11],[9,11],[3,11],[3,6],[1,2],[4,6],[6,11],[3,7],[6,7],[6,11],[2,10],[0,7],[3,4],[1,11],[0,2],[0,9],[1,8],[0,1],[0,8],[7,11],[5,6]],[[2,3],[5,10],[4,6],[0,8],[9,11],[3,6],[1,4],[6,8],[5,6],[0,4],[4,6],[5,11],[3,5],[3,5],[0,3],[0,10],[2,3],[0,4],[4,6],[2,4],[0,5],[1,3],[4,9],[0,4],[5,8],[6,11],[2,10],[8,11],[0,6],[7,10],[7,11],[4,9]],[[5,11],[2,9],[1,3],[1,7],[0,11],[1,10],[0,11],[1,11],[4,11],[8,9],[4,7],[1,7],[4,5],[1,9],[1,4],[8,9],[4,7],[4,10],[7,8],[0,4],[3,6],[5,9],[0,5],[6,11],[2,10],[1,2],[6,7],[0,2],[0,2],[3,6],[4,11],[3,11]],[[0,3],[3,6],[0,11],[2,3],[0,10],[0,2],[1,6],[6,8],[0,5],[3,9],[0,6],[4,11],[7,11],[3,8],[6,10],[1,5],[5,10],[6,10],[3,9],[2,11],[0,4],[2,4],[1,5],[6,10],[10,11],[2,9],[9,10],[1,6],[6,7],[1,5],[4,6],[6,7]],[[4,5],[1,2],[3,4],[3,5],[2,6],[7,11],[1,8],[2,5],[6,9],[3,7],[4,7],[4,7],[1,9],[5,10],[9,11],[3,7],[3,9],[1,3],[2,9],[0,3],[6,10],[0,6],[6,10],[8,10],[2,6],[7,9],[4,5],[10,11],[4,5],[4,11],[9,10],[2,11]],[[9,10],[5,10],[7,8],[6,10],[0,11],[7,8],[8,10],[10,11],[7,11],[9,10],[5,8],[3,6],[2,9],[10,11],[8,9],[4,5],[8,10],[3,10],[5,9],[2,5],[1,11],[1,5],[0,11],[6,10],[7,8],[3,5],[5,10],[8,11],[8,10],[8,10],[3,10],[2,7]]]
def setup_inputs(rng):
    return {"x": rng.standard_normal((N, 128, TOK), dtype=np.float32).astype(ml_dtypes.bfloat16), "gate": (0.5 * rng.integers(1, 4, size=(N, K, TOK)) * (2 * rng.integers(0, 2, size=(N, K, TOK)) - 1)).astype(np.float32).astype(ml_dtypes.bfloat16), "w1": (rng.standard_normal((N, 128, FT * 128), dtype=np.float32) / 8).astype(ml_dtypes.bfloat16), "w2": (rng.standard_normal((N, 128, FT * 128), dtype=np.float32) / 8).astype(ml_dtypes.bfloat16)}
def setup_inputs_big(rng):
    d = setup_inputs(rng)
    for k in ("x", "gate", "w1", "w2"): d[k] = (d[k].astype(np.float32) * 1024.0).astype(d[k].dtype)
    return d
def setup_inputs_small(rng):
    d = setup_inputs(rng)
    for k in ("x", "gate", "w1", "w2"): d[k] = (d[k].astype(np.float32) * (1 / 1024.0)).astype(d[k].dtype)
    return d
def reference(x, gate, w1, w2):
    X, GATE, W1, W2 = x.astype(np.float64), gate.astype(np.float64), w1.astype(np.float64), w2.astype(np.float64)
    y = np.zeros((N, 128, TOK))
    for r in range(N):
        for t in range(TOK):
            for i, e in enumerate(ROUTE[r][t]):
                hid = np.maximum(W1[e].T @ X[r][:, t], 0.0)
                y[r][:, t] += GATE[r][i, t] * sum(W2[e][:, 128 * f:128 * f + 128].T @ hid[128 * f:128 * f + 128] for f in range(FT))
    return {"y": y.astype(ml_dtypes.bfloat16)}

@@ -1,0 +1,353 @@
+from concourse.bass import DstId, RemoteDMATransfer
+from concourse.mybir import AluOpType
+
+BF, F32 = "bfloat16", "float32"
+SCRATCH = {
+    "xall": ("sbuf", [128, 384], BF),
+    "w1s": ("sbuf", [128, 512], BF),
+    "w2s": ("sbuf", [128, 512], BF),
+    "gsb": ("sbuf", [128, 64], BF),
+    "ones": ("sbuf", [128, 128], BF),
+    "zero": ("sbuf", [128, 256], BF),
+    "msk": ("sbuf", [128, 768], BF),
+    "h0": ("sbuf", [128, 512], BF),
+    "h1": ("sbuf", [128, 512], BF),
+    "h2": ("sbuf", [128, 512], BF),
+    "va": ("sbuf", [128, 4, 2, 32], BF),
+    "vb": ("sbuf", [128, 8, 2, 32], BF),
+    "landa": ("sbuf", [128, 3, 2, 32], BF),
+    "redl": ("sbuf", [128, 3, 3, 2, 32], BF),
+    "landb": ("sbuf", [128, 2, 2, 32], BF),
+    "a1": ("sbuf", [128, 2, 32], F32),
+    "a2": ("sbuf", [128, 2, 32], F32),
+    "a3": ("sbuf", [128, 2, 32], F32),
+    "a4": ("sbuf", [128, 2, 32], F32),
+    "a5": ("sbuf", [128, 2, 32], F32),
+    "tg": ("sbuf", [128, 2, 32], F32),
+    "ysb": ("sbuf", [128, 32], BF),
+    "z0": ("psum", [128, 512], F32),
+    "z1": ("psum", [128, 512], F32),
+    "z2": ("psum", [128, 512], F32),
+    "z3": ("psum", [128, 512], F32),
+    "r0": ("psum", [128, 512], F32),
+    "r1": ("psum", [128, 512], F32),
+    "r2": ("psum", [128, 512], F32),
+    "gp": ("psum", [128, 512], F32),
+}
+SEMAPHORES = (["ldx", "ldw1", "ldw2", "ldg", "st", "vz", "vo", "vm", "pg", "xin0", "xin1", "xin2",
+               "ya", "red", "yin0", "yin1", "hs", "sent"]
+              + ["pz%d%d" % (q, h) for q in range(3) for h in range(2)]
+              + ["ph%d%d" % (q, h) for q in range(3) for h in range(2)]
+              + ["pr%d" % q for q in range(3)] + ["pv%d" % q for q in range(3)])
+
+
+def pow2_floor(n):
+    p = 1
+    while p * 2 <= n:
+        p *= 2
+    return p
+
+
+def make_plan(cores, topo):
+    n = len(cores)
+    chips = []
+    for c in cores:
+        if topo.chip(c) not in chips:
+            chips.append(topo.chip(c))
+    nch = len(chips)
+    memb = [[r for r in range(n) if topo.chip(cores[r]) == ch] for ch in chips]
+    grp = len(memb[0])
+    for a in range(nch):
+        assert memb[a] == list(range(a * grp, (a + 1) * grp))
+    cidx = [chips.index(topo.chip(c)) for c in cores]
+    order = []
+    for a in range(nch):
+        oth = [b for b in range(nch) if b != a]
+        oth.sort(key=lambda b: 0 if topo.same_plane(chips[a], chips[b]) else 1)
+        order.append([a] + oth)
+    serve, far = {}, []
+    for a in range(nch):
+        homes = [r for b in order[a][1:] for r in memb[b]]
+        far.append(homes)
+        reach = {}
+        for s in memb[a]:
+            reach[s] = sum(1 for r in homes if topo.may_write(cores[s], cores[r]))
+        able = sorted([s for s in memb[a] if reach[s] > 0], key=lambda s: reach[s])
+        base, rem = divmod(len(homes), len(able))
+        p = 0
+        for j, s in enumerate(able):
+            w = base + (1 if j >= len(able) - rem else 0)
+            serve[s] = (p, p + w)
+            for r in homes[p:p + w]:
+                assert topo.may_write(cores[s], cores[r])
+            p += w
+        for s in memb[a]:
+            if s not in serve:
+                serve[s] = (0, 0)
+
+    def deal(src, trs):
+        avail = None
+        for t in trs:
+            for d in t["dst"]:
+                m = topo.mask(cores[src], cores[d])
+                avail = m if avail is None else (avail & m)
+        b = [e for e in range(avail.bit_length()) if (avail >> e) & 1]
+        per = pow2_floor(len(b) // len(trs))
+        for i, t in enumerate(trs):
+            t["mask"] = sum(1 << e for e in b[i * per:(i + 1) * per])
+            t["n"] = per
+        return trs
+
+    calls = {}
+    for s in range(n):
+        a = cidx[s]
+        us = s - memb[a][0]
+        peers = [r for r in memb[a] if r != s]
+        p0, p1 = serve[s]
+        c = {"p1": [], "p2": [], "p3a": [], "p3b": [], "p4": []}
+        c["p1"].append(deal(s, [{"kind": "x1", "dst": peers, "sem": "xin%d" % a}]))
+        if p1 > p0:
+            c["p2"].append(deal(s, [{"kind": "x2", "dst": far[a][p0:p1], "sem": "xin%d" % a}]))
+        trs = []
+        for d in peers:
+            ud = d - memb[a][0]
+            trs.append({"kind": "va", "dst": [d], "sem": "ya", "u": ud, "slot": us - (1 if us > ud else 0)})
+        c["p3a"].append(deal(s, trs))
+        groups = {}
+        for d in peers:
+            q0, q1 = serve[d]
+            if q1 > q0:
+                ud = d - memb[a][0]
+                key = ((q1 - 1) // grp + 1, q1 - q0)
+                groups.setdefault(key, []).append({"kind": "vb", "dst": [d], "sem": "red", "q0": q0, "q1": q1,
+                                                   "slot": us - (1 if us > ud else 0)})
+        for key in sorted(groups):
+            c["p3b"].append((key[0], deal(s, groups[key])))
+        trs = []
+        for p in range(p0, p1):
+            r = far[a][p]
+            trs.append({"kind": "fold", "dst": [r], "sem": "yin%d" % order[cidx[r]][1:].index(a), "p": p, "j": p - p0,
+                        "slot": order[cidx[r]][1:].index(a)})
+        while trs:
+            k = pow2_floor(len(trs))
+            c["p4"].append(deal(s, trs[:k]))
+            trs = trs[k:]
+        calls[s] = c
+
+    def flat(s):
+        c = calls[s]
+        out = []
+        for ph in ("p1", "p2", "p3a", "p4"):
+            for call in c[ph]:
+                out.extend(call)
+        for need, call in c["p3b"]:
+            out.extend(call)
+        return out
+
+    def expected(rank):
+        e = {}
+        for s in range(n):
+            for t in flat(s):
+                if rank in t["dst"]:
+                    e[t["sem"]] = e.get(t["sem"], 0) + t["n"]
+        return e
+
+    return {"chips": chips, "memb": memb, "grp": grp, "cidx": cidx, "order": order, "serve": serve, "calls": calls,
+            "flat": flat, "expected": expected}
+
+
+def rank_program(g, core, T, topo):
+    rank = T.rank_of(core)
+    if rank is None:
+        return
+    cores = list(T.cores)
+    tok, route = T.tables["TOK"], T.tables["ROUTE"]
+    n = len(cores)
+    plan = make_plan(cores, topo)
+    grp, a = plan["grp"], plan["cidx"][rank]
+    order = plan["order"][a]
+    u_own = rank - plan["memb"][a][0]
+    blk = grp * tok
+    ncol = n * tok
+    exp = plan["expected"](rank)
+    mine = plan["calls"][rank]
+    S = T.sem
+    pe, ve, sy, sc = g.tensor, g.vector, g.sync, g.scalar
+    tot = {}
+
+    def note(name, k):
+        tot[name] = tot.get(name, 0) + k
+
+    for name in exp:
+        note(name, exp[name])
+    note("sent", sum(t["n"] for t in plan["flat"](rank)))
+
+    sy.dma_start(T.xall[:, rank * tok:(rank + 1) * tok], T.x[:, :]).then_inc(S.ldx, 16)
+    sy.dma_start(T.w1s[:, :], T.w1[:, :]).then_inc(S.ldw1, 16)
+    sy.dma_start(T.w2s[:, :], T.w2[:, :]).then_inc(S.ldw2, 16)
+    sc.dma_start(T.gsb[0:1, 0:tok], T.gate[0:1, :]).then_inc(S.ldg, 16)
+    sc.dma_start(T.gsb[0:1, tok:2 * tok], T.gate[1:2, :]).then_inc(S.ldg, 16)
+    note("ldx", 16), note("ldw1", 16), note("ldw2", 16), note("ldg", 32)
+
+    ve.memset(T.ones[0:1, :], 1.0).then_inc(S.vo, 1)
+    ve.memset(T.zero[:, :], 0.0).then_inc(S.vz, 1)
+    ve.memset(T.msk[:, :], 0.0).then_inc(S.vm, 1)
+    ve.wait_ge(S.vm, 1)
+    note("vo", 1), note("vz", 1), note("vm", 1)
+    cols = sorted(i * ncol + r * tok + t for r in range(n) for t in range(tok) for i in range(len(route[r][t]))
+                  if route[r][t][i] == rank)
+    runs = []
+    for cc in cols:
+        if runs and runs[-1][1] == cc:
+            runs[-1][1] = cc + 1
+        else:
+            runs.append([cc, cc + 1])
+    for lo, hi in runs:
+        ve.memset(T.msk[:, lo:hi], 1.0).then_inc(S.vm, 1)
+        note("vm", 1)
+
+    def dst_of(r):
+        ad = topo.addr(cores[r])
+        return DstId(rid=ad[0], pnc=ad[1])
+
+    def emit(call):
+        trs = []
+        for t in call:
+            k, op = t["kind"], 0
+            if k == "x1":
+                src = [T.xall[:, rank * tok:(rank + 1) * tok]]
+                dst = T.xall[:, rank * tok:(rank + 1) * tok]
+            elif k == "x2":
+                src = [T.xall[:, a * blk:(a + 1) * blk]]
+                dst = T.xall[:, a * blk:(a + 1) * blk]
+            elif k == "va":
+                src = [T.va[:, t["u"]]]
+                dst = T.landa[:, t["slot"]]
+            elif k == "vb":
+                src = [T.vb[:, t["q0"]:t["q1"]]]
+                dst = T.redl[:, t["slot"], 0:t["q1"] - t["q0"]]
+            else:
+                src = [T.vb[:, t["p"]]] + [T.redl[:, s, t["j"]] for s in range(grp - 1)]
+                dst = T.landb[:, t["slot"]]
+                op = 1
+            trs.append(RemoteDMATransfer(dst_ids=[dst_of(r) for r in t["dst"]], dma_engine_mask=t["mask"],
+                                         remote_sem=S[t["sem"]], srcs=src, dsts=[dst for r in t["dst"]], alu_op=op))
+        g.remote_dma_fused(trs, local_sem=S.sent)
+
+    own_in = "xin%d" % a
+    g.wait_ge(S.ldx, 16)
+    for call in mine["p1"]:
+        emit(call)
+    if mine["p2"]:
+        g.wait_ge(S[own_in], exp[own_in])
+        for call in mine["p2"]:
+            emit(call)
+    g.wait_ge(S.pv0, 2)
+    for call in mine["p3a"]:
+        emit(call)
+    for need, call in mine["p3b"]:
+        for q in range(1, need + 1):
+            g.wait_ge(S["pv%d" % q], 2)
+        emit(call)
+    if mine["p4"]:
+        g.wait_ge(S.pv1, 2)
+        g.wait_ge(S.pv2, 2)
+        g.wait_ge(S.red, exp["red"])
+        for call in mine["p4"]:
+            emit(call)
+
+    zb = [T.z0, T.z1, T.z2, T.z3]
+    rb = [T.r0, T.r1, T.r2]
+    hb = [T.h0, T.h1, T.h2]
+
+    def pe_z(q):
+        c = order[q]
+        if q == 0:
+            pe.wait_ge(S.ldw1, 16)
+            pe.wait_ge(S.ldx, 16)
+        pe.wait_ge(S["xin%d" % c], exp["xin%d" % c])
+        for h in range(2):
+            for k in range(2):
+                f = 2 * h + k
+                pe.matmul(zb[(2 * q + h) % 4][:, k * blk:(k + 1) * blk], T.w1s[:, f * 128:(f + 1) * 128],
+                          T.xall[:, c * blk:(c + 1) * blk], True, True).then_inc(S["pz%d%d" % (q, h)], 1)
+                note("pz%d%d" % (q, h), 1)
+
+    def pe_r(q):
+        if q == 0:
+            pe.wait_ge(S.ldw2, 16)
+        for f in range(4):
+            if f % 2 == 0:
+                pe.wait_ge(S["ph%d%d" % (q, f // 2)], 1)
+            pe.matmul(rb[q][:, 0:blk], T.w2s[:, f * 128:(f + 1) * 128], hb[q][:, f * blk:(f + 1) * blk],
+                      f == 0, f == 3).then_inc(S["pr%d" % q], 1)
+            note("pr%d" % q, 1)
+
+    def ve_relu(q):
+        if q == 0:
+            ve.wait_ge(S.vz, 1)
+        for h in range(2):
+            ve.wait_ge(S["pz%d%d" % (q, h)], 2)
+            ve.tensor_tensor(hb[q][:, h * 2 * blk:(h + 1) * 2 * blk], zb[(2 * q + h) % 4][:, 0:2 * blk],
+                             T.zero[:, 0:2 * blk], AluOpType.max).then_inc(S["ph%d%d" % (q, h)], 1)
+            note("ph%d%d" % (q, h), 1)
+
+    def ve_mask(q):
+        c = order[q]
+        if q == 0:
+            ve.wait_ge(S.vm, tot["vm"])
+        ve.wait_ge(S["pr%d" % q], 4)
+        for i in range(2):
+            out = T.va[:, 0:grp, i, :] if q == 0 else T.vb[:, (q - 1) * grp:q * grp, i, :]
+            ve.tensor_tensor(out, rb[q][:, 0:blk], T.msk[:, i * ncol + c * blk:i * ncol + (c + 1) * blk],
+                             AluOpType.mult).then_inc(S["pv%d" % q], 1)
+            note("pv%d" % q, 1)
+
+    pe.wait_ge(S.vo, 1)
+    pe.wait_ge(S.ldg, 32)
+    pe.matmul(T.gp[:, 0:2 * tok], T.ones[0:1, :], T.gsb[0:1, :], True, True).then_inc(S.pg, 1)
+    note("pg", 1)
+
+    pe_z(0), pe_r(0)
+    ve_relu(0), ve_mask(0)
+    ch = plan["chips"]
+    together = topo.same_plane(ch[a], ch[order[1]]) == topo.same_plane(ch[a], ch[order[2]])
+    if together:
+        pe_z(1), pe_z(2), pe_r(1), pe_r(2)
+        ve_relu(1), ve_relu(2), ve_mask(1), ve_mask(2)
+    else:
+        pe_z(1), pe_r(1), pe_z(2), pe_r(2)
+        ve_relu(1), ve_mask(1), ve_relu(2), ve_mask(2)
+
+    hs = [0]
+
+    def vop(out, in0, in1, op):
+        ve.tensor_tensor(out, in0, in1, op).then_inc(S.hs, 1)
+        hs[0] += 1
+        note("hs", 1)
+
+    ve.wait_ge(S.pv0, 2)
+    ve.wait_ge(S.ya, exp["ya"])
+    vop(T.a1[:, :, :], T.va[:, u_own], T.landa[:, 0], AluOpType.add)
+    vop(T.a2[:, :, :], T.landa[:, 1], T.landa[:, 2], AluOpType.add)
+    ve.wait_ge(S.hs, hs[0])
+    vop(T.a3[:, :, :], T.a1[:, :, :], T.a2[:, :, :], AluOpType.add)
+    ve.wait_ge(S.hs, hs[0])
+    ve.wait_ge(S.yin0, exp["yin0"])
+    vop(T.a4[:, :, :], T.a3[:, :, :], T.landb[:, 0], AluOpType.add)
+    ve.wait_ge(S.hs, hs[0])
+    ve.wait_ge(S.yin1, exp["yin1"])
+    vop(T.a5[:, :, :], T.a4[:, :, :], T.landb[:, 1], AluOpType.add)
+    ve.wait_ge(S.hs, hs[0])
+    ve.wait_ge(S.pg, 1)
+    vop(T.tg[:, :, :], T.a5[:, :, :], T.gp[:, 0:2 * tok], AluOpType.mult)
+    ve.wait_ge(S.hs, hs[0])
+    vop(T.ysb[:, :], T.tg[:, 0, :], T.tg[:, 1, :], AluOpType.add)
+    sy.wait_ge(S.hs, hs[0])
+    sy.dma_start(T.y[:, :], T.ysb[:, :]).then_inc(S.st, 16)
+    note("st", 16)
+
+    for name in sorted(tot):
+        if name != "st" and tot[name] > 0:
+            g.wait_ge(S[name], tot[name])
+    g.wait_ge(S.st, 16)

@@ -1,29 +1,30 @@
 from concourse.bass import DstId, RemoteDMATransfer
-from concourse.mybir import AluOpType
+from concourse.mybir import AluOpType, ActivationFunctionType
 
 BF, F32 = "bfloat16", "float32"
 SCRATCH = {
-    "xall": ("sbuf", [128, 384], BF),
+    "xs": ("sbuf", [128, 40], BF),
+    "xall": ("sbuf", [128, 396], BF),
     "w1s": ("sbuf", [128, 512], BF),
     "w2s": ("sbuf", [128, 512], BF),
-    "gsb": ("sbuf", [128, 64], BF),
     "ones": ("sbuf", [128, 128], BF),
-    "zero": ("sbuf", [128, 256], BF),
-    "msk": ("sbuf", [128, 768], BF),
-    "h0": ("sbuf", [128, 512], BF),
-    "h1": ("sbuf", [128, 512], BF),
-    "h2": ("sbuf", [128, 512], BF),
-    "va": ("sbuf", [128, 4, 2, 32], BF),
-    "vb": ("sbuf", [128, 8, 2, 32], BF),
-    "landa": ("sbuf", [128, 3, 2, 32], BF),
-    "redl": ("sbuf", [128, 3, 3, 2, 32], BF),
-    "landb": ("sbuf", [128, 2, 2, 32], BF),
-    "a1": ("sbuf", [128, 2, 32], F32),
-    "a2": ("sbuf", [128, 2, 32], F32),
-    "a3": ("sbuf", [128, 2, 32], F32),
-    "a4": ("sbuf", [128, 2, 32], F32),
-    "a5": ("sbuf", [128, 2, 32], F32),
-    "tg": ("sbuf", [128, 2, 32], F32),
+    "zero": ("sbuf", [128, 264], BF),
+    "dg": ("sbuf", [128, 64], BF),
+    "sel": ("sbuf", [128, 396], BF),
+    "gs": ("sbuf", [128, 396], BF),
+    "gm": ("sbuf", [128, 396], BF),
+    "h0": ("sbuf", [128, 528], BF),
+    "h1": ("sbuf", [128, 528], BF),
+    "h2": ("sbuf", [128, 528], BF),
+    "va": ("sbuf", [128, 132], BF),
+    "vb": ("sbuf", [128, 264], BF),
+    "landa": ("sbuf", [128, 99], BF),
+    "redl": ("sbuf", [128, 297], BF),
+    "landb": ("sbuf", [128, 66], BF),
+    "a1": ("sbuf", [128, 32], F32),
+    "a2": ("sbuf", [128, 32], F32),
+    "a3": ("sbuf", [128, 32], F32),
+    "a4": ("sbuf", [128, 32], F32),
     "ysb": ("sbuf", [128, 32], BF),
     "z0": ("psum", [128, 512], F32),
     "z1": ("psum", [128, 512], F32),
@@ -32,13 +33,13 @@ SCRATCH = {
     "r0": ("psum", [128, 512], F32),
     "r1": ("psum", [128, 512], F32),
     "r2": ("psum", [128, 512], F32),
-    "gp": ("psum", [128, 512], F32),
+    "gmp": ("psum", [128, 512], F32),
 }
-SEMAPHORES = (["ldx", "ldw1", "ldw2", "ldg", "st", "vz", "vo", "vm", "pg", "xin0", "xin1", "xin2",
-               "ya", "red", "yin0", "yin1", "hs", "sent"]
+SEMAPHORES = (["ldx", "ldw1", "ldw2", "ldg", "ldo", "st", "vx", "vz", "vo", "vm", "vd", "xin0", "xin1", "xin2",
+               "gw0", "gw1", "gw2", "xr", "ya", "red", "yin0", "yin1", "hs", "sent"]
               + ["pz%d%d" % (q, h) for q in range(3) for h in range(2)]
               + ["ph%d%d" % (q, h) for q in range(3) for h in range(2)]
-              + ["pr%d" % q for q in range(3)] + ["pv%d" % q for q in range(3)])
+              + ["%s%d" % (p, q) for p in ("pr", "pv", "pt", "pm", "pc") for q in range(3)])
 
 
 def pow2_floor(n):
@@ -65,6 +66,10 @@ def make_plan(cores, topo):
         oth = [b for b in range(nch) if b != a]
         oth.sort(key=lambda b: 0 if topo.same_plane(chips[a], chips[b]) else 1)
         order.append([a] + oth)
+
+    def can(s, b):
+        return all(topo.may_write(cores[s], cores[r]) for r in memb[b])
+
     serve, far = {}, []
     for a in range(nch):
         homes = [r for b in order[a][1:] for r in memb[b]]
@@ -85,18 +90,64 @@ def make_plan(cores, topo):
             if s not in serve:
                 serve[s] = (0, 0)
 
-    def deal(src, trs):
+    def engines(src, t):
         avail = None
+        for d in t["dst"]:
+            m = topo.mask(cores[src], cores[d])
+            avail = m if avail is None else (avail & m)
+        return [e for e in range(avail.bit_length()) if (avail >> e) & 1]
+
+    def give(t, b):
+        b = b[:pow2_floor(len(b))]
+        t["mask"] = sum(1 << e for e in b)
+        t["n"] = len(b)
+
+    def deal(src, trs):
+        b = None
         for t in trs:
-            for d in t["dst"]:
-                m = topo.mask(cores[src], cores[d])
-                avail = m if avail is None else (avail & m)
-        b = [e for e in range(avail.bit_length()) if (avail >> e) & 1]
+            e = engines(src, t)
+            b = e if b is None else [x for x in b if x in e]
         per = pow2_floor(len(b) // len(trs))
         for i, t in enumerate(trs):
-            t["mask"] = sum(1 << e for e in b[i * per:(i + 1) * per])
-            t["n"] = per
+            give(t, b[i * per:(i + 1) * per])
         return trs
+
+    def deal_two(src, tfar, tnear):
+        bf = engines(src, tfar)
+        rest = [e for e in engines(src, tnear) if e not in bf]
+        if not rest:
+            return deal(src, [tfar, tnear])
+        give(tfar, bf)
+        give(tnear, rest)
+        return [tfar, tnear]
+
+    def relay_share(z):
+        a = cidx[z]
+        dests = [r for b in order[a][1:] if not can(z, b) for r in memb[b]]
+        if not dests:
+            return {}
+        rel = [p for p in memb[a] if p != z and all(topo.may_write(cores[p], cores[r]) for r in dests)]
+        base, rem = divmod(len(dests), len(rel))
+        out, p = {}, 0
+        for j, s in enumerate(rel):
+            w = base + (1 if j >= len(rel) - rem else 0)
+            if w:
+                out[s] = dests[p:p + w]
+            p += w
+        return out
+
+    load = {}
+    for s in range(n):
+        a = cidx[s]
+        load[s] = grp - 1 + sum(1 for b in order[a][1:] if can(s, b))
+        load[s] += sum(len(relay_share(z).get(s, [])) for z in memb[a] if z != s)
+    gate_of = {}
+    for a in range(nch):
+        for b in order[a][1:]:
+            if any(can(z, a) for z in memb[b]):
+                pick = min(memb[a], key=lambda r: (load[r], r))
+                gate_of[(b, a)] = pick
+                load[pick] += grp - 1
 
     calls = {}
     for s in range(n):
@@ -104,10 +155,28 @@ def make_plan(cores, topo):
         us = s - memb[a][0]
         peers = [r for r in memb[a] if r != s]
         p0, p1 = serve[s]
-        c = {"p1": [], "p2": [], "p3a": [], "p3b": [], "p4": []}
-        c["p1"].append(deal(s, [{"kind": "x1", "dst": peers, "sem": "xin%d" % a}]))
-        if p1 > p0:
-            c["p2"].append(deal(s, [{"kind": "x2", "dst": far[a][p0:p1], "sem": "xin%d" % a}]))
+        c = {"disp": [], "p3a": [], "p3b": [], "p4": []}
+        direct = [b for b in order[a][1:] if can(s, b)]
+        blocked = len(direct) < nch - 1
+        tnear = {"kind": "xs", "dst": peers, "sem": "xr" if blocked else "xin%d" % a}
+        tfar = {"kind": "xs", "dst": [gate_of[(a, b)] for b in direct], "sem": "gw%d" % a}
+        if blocked:
+            c["disp"].append((None, deal(s, [tnear])))
+            if direct:
+                c["disp"].append((None, deal(s, [tfar])))
+        else:
+            c["disp"].append((None, deal_two(s, tfar, tnear)))
+        for z in peers:
+            part = relay_share(z).get(s)
+            if part:
+                c["disp"].append(("xr", deal(s, [{"kind": "xf", "src": z, "cnt": 1, "dst": part,
+                                                  "sem": "xin%d" % a}])))
+        for b in order[a][1:]:
+            if gate_of.get((b, a)) == s:
+                zs = [z for z in memb[b] if can(z, a)]
+                assert zs == list(range(zs[0], zs[0] + len(zs)))
+                c["disp"].append(("gw%d" % b, deal(s, [{"kind": "xf", "src": zs[0], "cnt": len(zs), "dst": peers,
+                                                        "sem": "xin%d" % b}])))
         trs = []
         for d in peers:
             ud = d - memb[a][0]
@@ -137,7 +206,9 @@ def make_plan(cores, topo):
     def flat(s):
         c = calls[s]
         out = []
-        for ph in ("p1", "p2", "p3a", "p4"):
+        for w, call in c["disp"]:
+            out.extend(call)
+        for ph in ("p3a", "p4"):
             for call in c[ph]:
                 out.extend(call)
         for need, call in c["p3b"]:
@@ -167,8 +238,9 @@ def rank_program(g, core, T, topo):
     grp, a = plan["grp"], plan["cidx"][rank]
     order = plan["order"][a]
     u_own = rank - plan["memb"][a][0]
-    blk = grp * tok
-    ncol = n * tok
+    pw = tok + 1
+    blk = grp * pw
+    kg = 2 * tok
     exp = plan["expected"](rank)
     mine = plan["calls"][rank]
     S = T.sem
@@ -182,76 +254,92 @@ def rank_program(g, core, T, topo):
         note(name, exp[name])
     note("sent", sum(t["n"] for t in plan["flat"](rank)))
 
-    sy.dma_start(T.xall[:, rank * tok:(rank + 1) * tok], T.x[:, :]).then_inc(S.ldx, 16)
+    sy.dma_start(T.xs[:, 0:tok], T.x[:, :]).then_inc(S.ldx, 16)
+    sc.dma_start(T.xs[0:kg, tok:pw], T.gate[:, :]).then_inc(S.ldg, 16)
     sy.dma_start(T.w1s[:, :], T.w1[:, :]).then_inc(S.ldw1, 16)
     sy.dma_start(T.w2s[:, :], T.w2[:, :]).then_inc(S.ldw2, 16)
-    sc.dma_start(T.gsb[0:1, 0:tok], T.gate[0:1, :]).then_inc(S.ldg, 16)
-    sc.dma_start(T.gsb[0:1, tok:2 * tok], T.gate[1:2, :]).then_inc(S.ldg, 16)
-    note("ldx", 16), note("ldw1", 16), note("ldw2", 16), note("ldg", 32)
+    note("ldx", 16), note("ldw1", 16), note("ldw2", 16), note("ldg", 16)
 
-    ve.memset(T.ones[0:1, :], 1.0).then_inc(S.vo, 1)
+    ve.memset(T.xs[kg:128, tok:pw], 0.0).then_inc(S.vx, 1)
+    ve.memset(T.ones[0:kg, :], 1.0).then_inc(S.vo, 1)
+    ve.memset(T.sel[0:kg, :], 0.0).then_inc(S.vm, 1)
     ve.memset(T.zero[:, :], 0.0).then_inc(S.vz, 1)
-    ve.memset(T.msk[:, :], 0.0).then_inc(S.vm, 1)
-    ve.wait_ge(S.vm, 1)
-    note("vo", 1), note("vz", 1), note("vm", 1)
-    cols = sorted(i * ncol + r * tok + t for r in range(n) for t in range(tok) for i in range(len(route[r][t]))
+    note("vx", 1), note("vo", 1), note("vm", 1), note("vz", 1)
+    g.wait_ge(S.vo, 1)
+    g.affine_select(T.dg[0:kg, 0:kg], T.ones[0:kg, 0:kg], [[-tok, 2], [-1, tok]], AluOpType.is_equal, 0.0, 0,
+                    1).then_inc(S.vd, 1)
+    note("vd", 1)
+    sy.wait_ge(S.ldx, 16)
+    sy.wait_ge(S.ldg, 16)
+    sy.wait_ge(S.vx, 1)
+    sy.dma_start(T.xall[:, rank * pw:(rank + 1) * pw], T.xs[:, 0:pw]).then_inc(S.ldo, 16)
+    note("ldo", 16)
+    left = sorted((r * pw + t, tok * i + t) for r in range(n) for t in range(tok) for i in range(len(route[r][t]))
                   if route[r][t][i] == rank)
-    runs = []
-    for cc in cols:
-        if runs and runs[-1][1] == cc:
-            runs[-1][1] = cc + 1
+    ve.wait_ge(S.vm, 1)
+    ve.wait_ge(S.vd, 1)
+    while left:
+        c1, s1 = left.pop(0)
+        j = None
+        for k in range(len(left)):
+            if left[k][1] > s1:
+                j = k
+                break
+        if j is None:
+            ve.tensor_copy(T.sel[0:kg, c1:c1 + 1], T.dg[0:kg, s1:s1 + 1]).then_inc(S.vm, 1)
         else:
-            runs.append([cc, cc + 1])
-    for lo, hi in runs:
-        ve.memset(T.msk[:, lo:hi], 1.0).then_inc(S.vm, 1)
+            c2, s2 = left.pop(j)
+            ve.tensor_copy(T.sel[0:kg, c1:c2 + 1:c2 - c1], T.dg[0:kg, s1:s2 + 1:s2 - s1]).then_inc(S.vm, 1)
         note("vm", 1)
 
     def dst_of(r):
         ad = topo.addr(cores[r])
         return DstId(rid=ad[0], pnc=ad[1])
 
+    rw = (grp - 1) * pw
+
     def emit(call):
         trs = []
         for t in call:
             k, op = t["kind"], 0
-            if k == "x1":
-                src = [T.xall[:, rank * tok:(rank + 1) * tok]]
-                dst = T.xall[:, rank * tok:(rank + 1) * tok]
-            elif k == "x2":
-                src = [T.xall[:, a * blk:(a + 1) * blk]]
-                dst = T.xall[:, a * blk:(a + 1) * blk]
+            if k == "xs":
+                src = [T.xs[:, 0:pw]]
+                dst = T.xall[:, rank * pw:(rank + 1) * pw]
+            elif k == "xf":
+                src = [T.xall[:, t["src"] * pw:(t["src"] + t["cnt"]) * pw]]
+                dst = T.xall[:, t["src"] * pw:(t["src"] + t["cnt"]) * pw]
             elif k == "va":
-                src = [T.va[:, t["u"]]]
-                dst = T.landa[:, t["slot"]]
+                src = [T.va[:, t["u"] * pw:(t["u"] + 1) * pw]]
+                dst = T.landa[:, t["slot"] * pw:(t["slot"] + 1) * pw]
             elif k == "vb":
-                src = [T.vb[:, t["q0"]:t["q1"]]]
-                dst = T.redl[:, t["slot"], 0:t["q1"] - t["q0"]]
+                src = [T.vb[:, t["q0"] * pw:t["q1"] * pw]]
+                dst = T.redl[:, t["slot"] * rw:t["slot"] * rw + (t["q1"] - t["q0"]) * pw]
             else:
-                src = [T.vb[:, t["p"]]] + [T.redl[:, s, t["j"]] for s in range(grp - 1)]
-                dst = T.landb[:, t["slot"]]
+                src = [T.vb[:, t["p"] * pw:(t["p"] + 1) * pw]]
+                src += [T.redl[:, s * rw + t["j"] * pw:s * rw + (t["j"] + 1) * pw] for s in range(grp - 1)]
+                dst = T.landb[:, t["slot"] * pw:(t["slot"] + 1) * pw]
                 op = 1
             trs.append(RemoteDMATransfer(dst_ids=[dst_of(r) for r in t["dst"]], dma_engine_mask=t["mask"],
                                          remote_sem=S[t["sem"]], srcs=src, dsts=[dst for r in t["dst"]], alu_op=op))
         g.remote_dma_fused(trs, local_sem=S.sent)
 
-    own_in = "xin%d" % a
     g.wait_ge(S.ldx, 16)
-    for call in mine["p1"]:
+    g.wait_ge(S.ldg, 16)
+    g.wait_ge(S.vx, 1)
+    for w, call in mine["disp"]:
+        if w is not None:
+            g.wait_ge(S[w], exp[w])
         emit(call)
-    if mine["p2"]:
-        g.wait_ge(S[own_in], exp[own_in])
-        for call in mine["p2"]:
-            emit(call)
-    g.wait_ge(S.pv0, 2)
+    g.wait_ge(S.pv0, 1)
     for call in mine["p3a"]:
         emit(call)
     for need, call in mine["p3b"]:
         for q in range(1, need + 1):
-            g.wait_ge(S["pv%d" % q], 2)
+            g.wait_ge(S["pv%d" % q], 1)
         emit(call)
     if mine["p4"]:
-        g.wait_ge(S.pv1, 2)
-        g.wait_ge(S.pv2, 2)
+        for q in range(1, (plan["serve"][rank][1] - 1) // grp + 2):
+            g.wait_ge(S["pv%d" % q], 1)
         g.wait_ge(S.red, exp["red"])
         for call in mine["p4"]:
             emit(call)
@@ -260,18 +348,33 @@ def rank_program(g, core, T, topo):
     rb = [T.r0, T.r1, T.r2]
     hb = [T.h0, T.h1, T.h2]
 
+    def arrived(eng, c):
+        names = ["xin%d" % c, "gw%d" % c] + (["xr"] if c == a else [])
+        for nm in names:
+            if exp.get(nm, 0) > 0:
+                eng.wait_ge(S[nm], exp[nm])
+        if c == a:
+            eng.wait_ge(S.ldo, 16)
+
     def pe_z(q):
         c = order[q]
         if q == 0:
             pe.wait_ge(S.ldw1, 16)
-            pe.wait_ge(S.ldx, 16)
-        pe.wait_ge(S["xin%d" % c], exp["xin%d" % c])
+        arrived(pe, c)
         for h in range(2):
             for k in range(2):
                 f = 2 * h + k
                 pe.matmul(zb[(2 * q + h) % 4][:, k * blk:(k + 1) * blk], T.w1s[:, f * 128:(f + 1) * 128],
                           T.xall[:, c * blk:(c + 1) * blk], True, True).then_inc(S["pz%d%d" % (q, h)], 1)
                 note("pz%d%d" % (q, h), 1)
+        if q == 0:
+            pe.wait_ge(S.vo, 1)
+        else:
+            pe.wait_ge(S["pc%d" % (q - 1)], 1)
+        pe.wait_ge(S["pt%d" % q], grp)
+        pe.matmul(T.gmp[:, q * blk:(q + 1) * blk], T.ones[0:kg, :], T.gs[0:kg, c * blk:(c + 1) * blk],
+                  True, True).then_inc(S["pm%d" % q], 1)
+        note("pm%d" % q, 1)
 
     def pe_r(q):
         if q == 0:
@@ -283,66 +386,70 @@ def rank_program(g, core, T, topo):
                       f == 0, f == 3).then_inc(S["pr%d" % q], 1)
             note("pr%d" % q, 1)
 
-    def ve_relu(q):
-        if q == 0:
-            ve.wait_ge(S.vz, 1)
-        for h in range(2):
-            ve.wait_ge(S["pz%d%d" % (q, h)], 2)
-            ve.tensor_tensor(hb[q][:, h * 2 * blk:(h + 1) * 2 * blk], zb[(2 * q + h) % 4][:, 0:2 * blk],
-                             T.zero[:, 0:2 * blk], AluOpType.max).then_inc(S["ph%d%d" % (q, h)], 1)
-            note("ph%d%d" % (q, h), 1)
+    def sc_relu(q):
+        sc.wait_ge(S["pz%d0" % q], 2)
+        sc.activation(hb[q][:, 0:2 * blk], zb[(2 * q) % 4][:, 0:2 * blk],
+                      ActivationFunctionType.Relu).then_inc(S["ph%d0" % q], 1)
+        note("ph%d0" % q, 1)
 
-    def ve_mask(q):
+    def ve_head(q):
         c = order[q]
         if q == 0:
             ve.wait_ge(S.vm, tot["vm"])
-        ve.wait_ge(S["pr%d" % q], 4)
-        for i in range(2):
-            out = T.va[:, 0:grp, i, :] if q == 0 else T.vb[:, (q - 1) * grp:q * grp, i, :]
-            ve.tensor_tensor(out, rb[q][:, 0:blk], T.msk[:, i * ncol + c * blk:i * ncol + (c + 1) * blk],
-                             AluOpType.mult).then_inc(S["pv%d" % q], 1)
-            note("pv%d" % q, 1)
+            ve.wait_ge(S.vz, 1)
+        arrived(ve, c)
+        for r in plan["memb"][c]:
+            ve.tensor_scalar(T.gs[0:kg, r * pw:(r + 1) * pw], T.sel[0:kg, r * pw:(r + 1) * pw],
+                             T.xall[0:kg, r * pw + tok:(r + 1) * pw], None, AluOpType.mult).then_inc(S["pt%d" % q], 1)
+            note("pt%d" % q, 1)
+        ve.wait_ge(S["pz%d1" % q], 2)
+        ve.tensor_tensor(hb[q][:, 2 * blk:4 * blk], zb[(2 * q + 1) % 4][:, 0:2 * blk], T.zero[:, 0:2 * blk],
+                         AluOpType.max).then_inc(S["ph%d1" % q], 1)
+        note("ph%d1" % q, 1)
+        ve.wait_ge(S["pm%d" % q], 1)
+        ve.tensor_copy(T.gm[:, c * blk:(c + 1) * blk], T.gmp[:, q * blk:(q + 1) * blk]).then_inc(S["pc%d" % q], 1)
+        note("pc%d" % q, 1)
 
-    pe.wait_ge(S.vo, 1)
-    pe.wait_ge(S.ldg, 32)
-    pe.matmul(T.gp[:, 0:2 * tok], T.ones[0:1, :], T.gsb[0:1, :], True, True).then_inc(S.pg, 1)
-    note("pg", 1)
+    def ve_tail(q):
+        c = order[q]
+        ve.wait_ge(S["pc%d" % q], 1)
+        ve.wait_ge(S["pr%d" % q], 4)
+        out = T.va[:, 0:blk] if q == 0 else T.vb[:, (q - 1) * blk:q * blk]
+        ve.tensor_tensor(out, rb[q][:, 0:blk], T.gm[:, c * blk:(c + 1) * blk],
+                         AluOpType.mult).then_inc(S["pv%d" % q], 1)
+        note("pv%d" % q, 1)
 
     pe_z(0), pe_r(0)
-    ve_relu(0), ve_mask(0)
+    sc_relu(0), sc_relu(1), sc_relu(2)
+    ve_head(0), ve_tail(0)
     ch = plan["chips"]
     together = topo.same_plane(ch[a], ch[order[1]]) == topo.same_plane(ch[a], ch[order[2]])
     if together:
         pe_z(1), pe_z(2), pe_r(1), pe_r(2)
-        ve_relu(1), ve_relu(2), ve_mask(1), ve_mask(2)
+        ve_head(1), ve_head(2), ve_tail(1), ve_tail(2)
     else:
         pe_z(1), pe_r(1), pe_z(2), pe_r(2)
-        ve_relu(1), ve_mask(1), ve_relu(2), ve_mask(2)
+        ve_head(1), ve_tail(1), ve_head(2), ve_tail(2)
 
     hs = [0]
 
-    def vop(out, in0, in1, op):
-        ve.tensor_tensor(out, in0, in1, op).then_inc(S.hs, 1)
+    def vop(out, in0, in1):
+        ve.tensor_tensor(out, in0, in1, AluOpType.add).then_inc(S.hs, 1)
         hs[0] += 1
         note("hs", 1)
 
-    ve.wait_ge(S.pv0, 2)
+    ve.wait_ge(S.pv0, 1)
     ve.wait_ge(S.ya, exp["ya"])
-    vop(T.a1[:, :, :], T.va[:, u_own], T.landa[:, 0], AluOpType.add)
-    vop(T.a2[:, :, :], T.landa[:, 1], T.landa[:, 2], AluOpType.add)
+    vop(T.a1[:, :], T.va[:, u_own * pw:u_own * pw + tok], T.landa[:, 0:tok])
+    vop(T.a2[:, :], T.landa[:, pw:pw + tok], T.landa[:, 2 * pw:2 * pw + tok])
     ve.wait_ge(S.hs, hs[0])
-    vop(T.a3[:, :, :], T.a1[:, :, :], T.a2[:, :, :], AluOpType.add)
+    vop(T.a3[:, :], T.a1[:, :], T.a2[:, :])
     ve.wait_ge(S.hs, hs[0])
     ve.wait_ge(S.yin0, exp["yin0"])
-    vop(T.a4[:, :, :], T.a3[:, :, :], T.landb[:, 0], AluOpType.add)
+    vop(T.a4[:, :], T.a3[:, :], T.landb[:, 0:tok])
     ve.wait_ge(S.hs, hs[0])
     ve.wait_ge(S.yin1, exp["yin1"])
-    vop(T.a5[:, :, :], T.a4[:, :, :], T.landb[:, 1], AluOpType.add)
-    ve.wait_ge(S.hs, hs[0])
-    ve.wait_ge(S.pg, 1)
-    vop(T.tg[:, :, :], T.a5[:, :, :], T.gp[:, 0:2 * tok], AluOpType.mult)
-    ve.wait_ge(S.hs, hs[0])
-    vop(T.ysb[:, :], T.tg[:, 0, :], T.tg[:, 1, :], AluOpType.add)
+    vop(T.ysb[:, :], T.a4[:, :], T.landb[:, pw:pw + tok])
     sy.wait_ge(S.hs, hs[0])
     sy.dma_start(T.y[:, :], T.ysb[:, :]).then_inc(S.st, 16)
     note("st", 16)

from concourse.bass import DstId, RemoteDMATransfer
from concourse.mybir import AluOpType, ActivationFunctionType

BF, F32 = "bfloat16", "float32"
SCRATCH = {
    "xs": ("sbuf", [128, 40], BF),
    "xall": ("sbuf", [128, 396], BF),
    "w1s": ("sbuf", [128, 512], BF),
    "w2s": ("sbuf", [128, 512], BF),
    "ones": ("sbuf", [128, 128], BF),
    "zero": ("sbuf", [128, 264], BF),
    "dg": ("sbuf", [128, 64], BF),
    "sel": ("sbuf", [128, 396], BF),
    "gs": ("sbuf", [128, 396], BF),
    "gm": ("sbuf", [128, 396], BF),
    "h0": ("sbuf", [128, 528], BF),
    "h1": ("sbuf", [128, 528], BF),
    "h2": ("sbuf", [128, 528], BF),
    "va": ("sbuf", [128, 132], BF),
    "vb": ("sbuf", [128, 264], BF),
    "landa": ("sbuf", [128, 99], BF),
    "redl": ("sbuf", [128, 297], BF),
    "landb": ("sbuf", [128, 66], BF),
    "a1": ("sbuf", [128, 32], F32),
    "a2": ("sbuf", [128, 32], F32),
    "a3": ("sbuf", [128, 32], F32),
    "a4": ("sbuf", [128, 32], F32),
    "ysb": ("sbuf", [128, 32], BF),
    "z0": ("psum", [128, 512], F32),
    "z1": ("psum", [128, 512], F32),
    "z2": ("psum", [128, 512], F32),
    "z3": ("psum", [128, 512], F32),
    "r0": ("psum", [128, 512], F32),
    "r1": ("psum", [128, 512], F32),
    "r2": ("psum", [128, 512], F32),
    "gmp": ("psum", [128, 512], F32),
}
SEMAPHORES = (["ldx", "ldw1", "ldw2", "ldg", "ldo", "st", "vx", "vz", "vo", "vm", "vd", "xin0", "xin1", "xin2",
               "gw0", "gw1", "gw2", "xr", "ya", "red", "yin0", "yin1", "hs", "sent"]
              + ["pz%d%d" % (q, h) for q in range(3) for h in range(2)]
              + ["ph%d%d" % (q, h) for q in range(3) for h in range(2)]
              + ["%s%d" % (p, q) for p in ("pr", "pv", "pt", "pm", "pc") for q in range(3)])


def pow2_floor(n):
    p = 1
    while p * 2 <= n:
        p *= 2
    return p


def make_plan(cores, topo):
    n = len(cores)
    chips = []
    for c in cores:
        if topo.chip(c) not in chips:
            chips.append(topo.chip(c))
    nch = len(chips)
    memb = [[r for r in range(n) if topo.chip(cores[r]) == ch] for ch in chips]
    grp = len(memb[0])
    for a in range(nch):
        assert memb[a] == list(range(a * grp, (a + 1) * grp))
    cidx = [chips.index(topo.chip(c)) for c in cores]
    order = []
    for a in range(nch):
        oth = [b for b in range(nch) if b != a]
        oth.sort(key=lambda b: 0 if topo.same_plane(chips[a], chips[b]) else 1)
        order.append([a] + oth)

    def can(s, b):
        return all(topo.may_write(cores[s], cores[r]) for r in memb[b])

    serve, far = {}, []
    for a in range(nch):
        homes = [r for b in order[a][1:] for r in memb[b]]
        far.append(homes)
        reach = {}
        for s in memb[a]:
            reach[s] = sum(1 for r in homes if topo.may_write(cores[s], cores[r]))
        able = sorted([s for s in memb[a] if reach[s] > 0], key=lambda s: reach[s])
        base, rem = divmod(len(homes), len(able))
        p = 0
        for j, s in enumerate(able):
            w = base + (1 if j >= len(able) - rem else 0)
            serve[s] = (p, p + w)
            for r in homes[p:p + w]:
                assert topo.may_write(cores[s], cores[r])
            p += w
        for s in memb[a]:
            if s not in serve:
                serve[s] = (0, 0)

    def engines(src, t):
        avail = None
        for d in t["dst"]:
            m = topo.mask(cores[src], cores[d])
            avail = m if avail is None else (avail & m)
        return [e for e in range(avail.bit_length()) if (avail >> e) & 1]

    def give(t, b):
        b = b[:pow2_floor(len(b))]
        t["mask"] = sum(1 << e for e in b)
        t["n"] = len(b)

    def deal(src, trs):
        b = None
        for t in trs:
            e = engines(src, t)
            b = e if b is None else [x for x in b if x in e]
        per = pow2_floor(len(b) // len(trs))
        for i, t in enumerate(trs):
            give(t, b[i * per:(i + 1) * per])
        return trs

    def deal_two(src, tfar, tnear):
        bf = engines(src, tfar)
        rest = [e for e in engines(src, tnear) if e not in bf]
        if not rest:
            return deal(src, [tfar, tnear])
        give(tfar, bf)
        give(tnear, rest)
        return [tfar, tnear]

    def relay_share(z):
        a = cidx[z]
        dests = [r for b in order[a][1:] if not can(z, b) for r in memb[b]]
        if not dests:
            return {}
        rel = [p for p in memb[a] if p != z and all(topo.may_write(cores[p], cores[r]) for r in dests)]
        base, rem = divmod(len(dests), len(rel))
        out, p = {}, 0
        for j, s in enumerate(rel):
            w = base + (1 if j >= len(rel) - rem else 0)
            if w:
                out[s] = dests[p:p + w]
            p += w
        return out

    load = {}
    for s in range(n):
        a = cidx[s]
        load[s] = grp - 1 + sum(1 for b in order[a][1:] if can(s, b))
        load[s] += sum(len(relay_share(z).get(s, [])) for z in memb[a] if z != s)
    gate_of = {}
    for a in range(nch):
        for b in order[a][1:]:
            if any(can(z, a) for z in memb[b]):
                pick = min(memb[a], key=lambda r: (load[r], r))
                gate_of[(b, a)] = pick
                load[pick] += grp - 1

    calls = {}
    for s in range(n):
        a = cidx[s]
        us = s - memb[a][0]
        peers = [r for r in memb[a] if r != s]
        p0, p1 = serve[s]
        c = {"disp": [], "p3a": [], "p3b": [], "p4": []}
        direct = [b for b in order[a][1:] if can(s, b)]
        blocked = len(direct) < nch - 1
        tnear = {"kind": "xs", "dst": peers, "sem": "xr" if blocked else "xin%d" % a}
        tfar = {"kind": "xs", "dst": [gate_of[(a, b)] for b in direct], "sem": "gw%d" % a}
        if blocked:
            c["disp"].append((None, deal(s, [tnear])))
            if direct:
                c["disp"].append((None, deal(s, [tfar])))
        else:
            c["disp"].append((None, deal_two(s, tfar, tnear)))
        for z in peers:
            part = relay_share(z).get(s)
            if part:
                c["disp"].append(("xr", deal(s, [{"kind": "xf", "src": z, "cnt": 1, "dst": part,
                                                  "sem": "xin%d" % a}])))
        for b in order[a][1:]:
            if gate_of.get((b, a)) == s:
                zs = [z for z in memb[b] if can(z, a)]
                assert zs == list(range(zs[0], zs[0] + len(zs)))
                c["disp"].append(("gw%d" % b, deal(s, [{"kind": "xf", "src": zs[0], "cnt": len(zs), "dst": peers,
                                                        "sem": "xin%d" % b}])))
        trs = []
        for d in peers:
            ud = d - memb[a][0]
            trs.append({"kind": "va", "dst": [d], "sem": "ya", "u": ud, "slot": us - (1 if us > ud else 0)})
        c["p3a"].append(deal(s, trs))
        groups = {}
        for d in peers:
            q0, q1 = serve[d]
            if q1 > q0:
                ud = d - memb[a][0]
                key = ((q1 - 1) // grp + 1, q1 - q0)
                groups.setdefault(key, []).append({"kind": "vb", "dst": [d], "sem": "red", "q0": q0, "q1": q1,
                                                   "slot": us - (1 if us > ud else 0)})
        for key in sorted(groups):
            c["p3b"].append((key[0], deal(s, groups[key])))
        trs = []
        for p in range(p0, p1):
            r = far[a][p]
            trs.append({"kind": "fold", "dst": [r], "sem": "yin%d" % order[cidx[r]][1:].index(a), "p": p, "j": p - p0,
                        "slot": order[cidx[r]][1:].index(a)})
        while trs:
            k = pow2_floor(len(trs))
            c["p4"].append(deal(s, trs[:k]))
            trs = trs[k:]
        calls[s] = c

    def flat(s):
        c = calls[s]
        out = []
        for w, call in c["disp"]:
            out.extend(call)
        for ph in ("p3a", "p4"):
            for call in c[ph]:
                out.extend(call)
        for need, call in c["p3b"]:
            out.extend(call)
        return out

    def expected(rank):
        e = {}
        for s in range(n):
            for t in flat(s):
                if rank in t["dst"]:
                    e[t["sem"]] = e.get(t["sem"], 0) + t["n"]
        return e

    return {"chips": chips, "memb": memb, "grp": grp, "cidx": cidx, "order": order, "serve": serve, "calls": calls,
            "flat": flat, "expected": expected}


def rank_program(g, core, T, topo):
    rank = T.rank_of(core)
    if rank is None:
        return
    cores = list(T.cores)
    tok, route = T.tables["TOK"], T.tables["ROUTE"]
    n = len(cores)
    plan = make_plan(cores, topo)
    grp, a = plan["grp"], plan["cidx"][rank]
    order = plan["order"][a]
    u_own = rank - plan["memb"][a][0]
    pw = tok + 1
    blk = grp * pw
    kg = 2 * tok
    exp = plan["expected"](rank)
    mine = plan["calls"][rank]
    S = T.sem
    pe, ve, sy, sc = g.tensor, g.vector, g.sync, g.scalar
    tot = {}

    def note(name, k):
        tot[name] = tot.get(name, 0) + k

    for name in exp:
        note(name, exp[name])
    note("sent", sum(t["n"] for t in plan["flat"](rank)))

    sy.dma_start(T.xs[:, 0:tok], T.x[:, :]).then_inc(S.ldx, 16)
    sc.dma_start(T.xs[0:kg, tok:pw], T.gate[:, :]).then_inc(S.ldg, 16)
    sy.dma_start(T.w1s[:, :], T.w1[:, :]).then_inc(S.ldw1, 16)
    sy.dma_start(T.w2s[:, :], T.w2[:, :]).then_inc(S.ldw2, 16)
    note("ldx", 16), note("ldw1", 16), note("ldw2", 16), note("ldg", 16)

    ve.memset(T.xs[kg:128, tok:pw], 0.0).then_inc(S.vx, 1)
    ve.memset(T.ones[0:kg, :], 1.0).then_inc(S.vo, 1)
    ve.memset(T.sel[0:kg, :], 0.0).then_inc(S.vm, 1)
    ve.memset(T.zero[:, :], 0.0).then_inc(S.vz, 1)
    note("vx", 1), note("vo", 1), note("vm", 1), note("vz", 1)
    g.wait_ge(S.vo, 1)
    g.affine_select(T.dg[0:kg, 0:kg], T.ones[0:kg, 0:kg], [[-tok, 2], [-1, tok]], AluOpType.is_equal, 0.0, 0,
                    1).then_inc(S.vd, 1)
    note("vd", 1)
    sy.wait_ge(S.ldx, 16)
    sy.wait_ge(S.ldg, 16)
    sy.wait_ge(S.vx, 1)
    sy.dma_start(T.xall[:, rank * pw:(rank + 1) * pw], T.xs[:, 0:pw]).then_inc(S.ldo, 16)
    note("ldo", 16)
    left = sorted((r * pw + t, tok * i + t) for r in range(n) for t in range(tok) for i in range(len(route[r][t]))
                  if route[r][t][i] == rank)
    ve.wait_ge(S.vm, 1)
    ve.wait_ge(S.vd, 1)
    while left:
        c1, s1 = left.pop(0)
        j = None
        for k in range(len(left)):
            if left[k][1] > s1:
                j = k
                break
        if j is None:
            ve.tensor_copy(T.sel[0:kg, c1:c1 + 1], T.dg[0:kg, s1:s1 + 1]).then_inc(S.vm, 1)
        else:
            c2, s2 = left.pop(j)
            ve.tensor_copy(T.sel[0:kg, c1:c2 + 1:c2 - c1], T.dg[0:kg, s1:s2 + 1:s2 - s1]).then_inc(S.vm, 1)
        note("vm", 1)

    def dst_of(r):
        ad = topo.addr(cores[r])
        return DstId(rid=ad[0], pnc=ad[1])

    rw = (grp - 1) * pw

    def emit(call):
        trs = []
        for t in call:
            k, op = t["kind"], 0
            if k == "xs":
                src = [T.xs[:, 0:pw]]
                dst = T.xall[:, rank * pw:(rank + 1) * pw]
            elif k == "xf":
                src = [T.xall[:, t["src"] * pw:(t["src"] + t["cnt"]) * pw]]
                dst = T.xall[:, t["src"] * pw:(t["src"] + t["cnt"]) * pw]
            elif k == "va":
                src = [T.va[:, t["u"] * pw:(t["u"] + 1) * pw]]
                dst = T.landa[:, t["slot"] * pw:(t["slot"] + 1) * pw]
            elif k == "vb":
                src = [T.vb[:, t["q0"] * pw:t["q1"] * pw]]
                dst = T.redl[:, t["slot"] * rw:t["slot"] * rw + (t["q1"] - t["q0"]) * pw]
            else:
                src = [T.vb[:, t["p"] * pw:(t["p"] + 1) * pw]]
                src += [T.redl[:, s * rw + t["j"] * pw:s * rw + (t["j"] + 1) * pw] for s in range(grp - 1)]
                dst = T.landb[:, t["slot"] * pw:(t["slot"] + 1) * pw]
                op = 1
            trs.append(RemoteDMATransfer(dst_ids=[dst_of(r) for r in t["dst"]], dma_engine_mask=t["mask"],
                                         remote_sem=S[t["sem"]], srcs=src, dsts=[dst for r in t["dst"]], alu_op=op))
        g.remote_dma_fused(trs, local_sem=S.sent)

    g.wait_ge(S.ldx, 16)
    g.wait_ge(S.ldg, 16)
    g.wait_ge(S.vx, 1)
    for w, call in mine["disp"]:
        if w is not None:
            g.wait_ge(S[w], exp[w])
        emit(call)
    g.wait_ge(S.pv0, 1)
    for call in mine["p3a"]:
        emit(call)
    for need, call in mine["p3b"]:
        for q in range(1, need + 1):
            g.wait_ge(S["pv%d" % q], 1)
        emit(call)
    if mine["p4"]:
        for q in range(1, (plan["serve"][rank][1] - 1) // grp + 2):
            g.wait_ge(S["pv%d" % q], 1)
        g.wait_ge(S.red, exp["red"])
        for call in mine["p4"]:
            emit(call)

    zb = [T.z0, T.z1, T.z2, T.z3]
    rb = [T.r0, T.r1, T.r2]
    hb = [T.h0, T.h1, T.h2]

    def arrived(eng, c):
        names = ["xin%d" % c, "gw%d" % c] + (["xr"] if c == a else [])
        for nm in names:
            if exp.get(nm, 0) > 0:
                eng.wait_ge(S[nm], exp[nm])
        if c == a:
            eng.wait_ge(S.ldo, 16)

    def pe_z(q):
        c = order[q]
        if q == 0:
            pe.wait_ge(S.ldw1, 16)
        arrived(pe, c)
        for h in range(2):
            for k in range(2):
                f = 2 * h + k
                pe.matmul(zb[(2 * q + h) % 4][:, k * blk:(k + 1) * blk], T.w1s[:, f * 128:(f + 1) * 128],
                          T.xall[:, c * blk:(c + 1) * blk], True, True).then_inc(S["pz%d%d" % (q, h)], 1)
                note("pz%d%d" % (q, h), 1)
        if q == 0:
            pe.wait_ge(S.vo, 1)
        else:
            pe.wait_ge(S["pc%d" % (q - 1)], 1)
        pe.wait_ge(S["pt%d" % q], grp)
        pe.matmul(T.gmp[:, q * blk:(q + 1) * blk], T.ones[0:kg, :], T.gs[0:kg, c * blk:(c + 1) * blk],
                  True, True).then_inc(S["pm%d" % q], 1)
        note("pm%d" % q, 1)

    def pe_r(q):
        if q == 0:
            pe.wait_ge(S.ldw2, 16)
        for f in range(4):
            if f % 2 == 0:
                pe.wait_ge(S["ph%d%d" % (q, f // 2)], 1)
            pe.matmul(rb[q][:, 0:blk], T.w2s[:, f * 128:(f + 1) * 128], hb[q][:, f * blk:(f + 1) * blk],
                      f == 0, f == 3).then_inc(S["pr%d" % q], 1)
            note("pr%d" % q, 1)

    def sc_relu(q):
        sc.wait_ge(S["pz%d0" % q], 2)
        sc.activation(hb[q][:, 0:2 * blk], zb[(2 * q) % 4][:, 0:2 * blk],
                      ActivationFunctionType.Relu).then_inc(S["ph%d0" % q], 1)
        note("ph%d0" % q, 1)

    def ve_head(q):
        c = order[q]
        if q == 0:
            ve.wait_ge(S.vm, tot["vm"])
            ve.wait_ge(S.vz, 1)
        arrived(ve, c)
        for r in plan["memb"][c]:
            ve.tensor_scalar(T.gs[0:kg, r * pw:(r + 1) * pw], T.sel[0:kg, r * pw:(r + 1) * pw],
                             T.xall[0:kg, r * pw + tok:(r + 1) * pw], None, AluOpType.mult).then_inc(S["pt%d" % q], 1)
            note("pt%d" % q, 1)
        ve.wait_ge(S["pz%d1" % q], 2)
        ve.tensor_tensor(hb[q][:, 2 * blk:4 * blk], zb[(2 * q + 1) % 4][:, 0:2 * blk], T.zero[:, 0:2 * blk],
                         AluOpType.max).then_inc(S["ph%d1" % q], 1)
        note("ph%d1" % q, 1)
        ve.wait_ge(S["pm%d" % q], 1)
        ve.tensor_copy(T.gm[:, c * blk:(c + 1) * blk], T.gmp[:, q * blk:(q + 1) * blk]).then_inc(S["pc%d" % q], 1)
        note("pc%d" % q, 1)

    def ve_tail(q):
        c = order[q]
        ve.wait_ge(S["pc%d" % q], 1)
        ve.wait_ge(S["pr%d" % q], 4)
        out = T.va[:, 0:blk] if q == 0 else T.vb[:, (q - 1) * blk:q * blk]
        ve.tensor_tensor(out, rb[q][:, 0:blk], T.gm[:, c * blk:(c + 1) * blk],
                         AluOpType.mult).then_inc(S["pv%d" % q], 1)
        note("pv%d" % q, 1)

    pe_z(0), pe_r(0)
    sc_relu(0), sc_relu(1), sc_relu(2)
    ve_head(0), ve_tail(0)
    ch = plan["chips"]
    together = topo.same_plane(ch[a], ch[order[1]]) == topo.same_plane(ch[a], ch[order[2]])
    if together:
        pe_z(1), pe_z(2), pe_r(1), pe_r(2)
        ve_head(1), ve_head(2), ve_tail(1), ve_tail(2)
    else:
        pe_z(1), pe_r(1), pe_z(2), pe_r(2)
        ve_head(1), ve_tail(1), ve_head(2), ve_tail(2)

    hs = [0]

    def vop(out, in0, in1):
        ve.tensor_tensor(out, in0, in1, AluOpType.add).then_inc(S.hs, 1)
        hs[0] += 1
        note("hs", 1)

    ve.wait_ge(S.pv0, 1)
    ve.wait_ge(S.ya, exp["ya"])
    vop(T.a1[:, :], T.va[:, u_own * pw:u_own * pw + tok], T.landa[:, 0:tok])
    vop(T.a2[:, :], T.landa[:, pw:pw + tok], T.landa[:, 2 * pw:2 * pw + tok])
    ve.wait_ge(S.hs, hs[0])
    vop(T.a3[:, :], T.a1[:, :], T.a2[:, :])
    ve.wait_ge(S.hs, hs[0])
    ve.wait_ge(S.yin0, exp["yin0"])
    vop(T.a4[:, :], T.a3[:, :], T.landb[:, 0:tok])
    ve.wait_ge(S.hs, hs[0])
    ve.wait_ge(S.yin1, exp["yin1"])
    vop(T.ysb[:, :], T.a4[:, :], T.landb[:, pw:pw + tok])
    sy.wait_ge(S.hs, hs[0])
    sy.dma_start(T.y[:, :], T.ysb[:, :]).then_inc(S.st, 16)
    note("st", 16)

    for name in sorted(tot):
        if name != "st" and tot[name] > 0:
            g.wait_ge(S[name], tot[name])
    g.wait_ge(S.st, 16)
